import numpy as np
import ml_dtypes


def mxq(x, axis, fmt="e4m3"):
    dtype, down = {"e4m3": (ml_dtypes.float8_e4m3fn, 7), "e5m2": (ml_dtypes.float8_e5m2, 14)}[fmt]
    v = np.moveaxis(np.asarray(x, np.float32).astype(ml_dtypes.bfloat16).astype(np.float64), axis, -1)
    blocks = v.reshape(v.shape[:-1] + (-1, 32))
    amax = np.abs(blocks).max(-1, keepdims=True)
    byte = np.maximum(np.where(amax > 0, np.frexp(amax)[1] - 1 + 127, 0) - down, 1)
    scale = np.exp2(byte - 127.0)
    codes = (blocks / scale).astype(np.float32).astype(dtype).astype(np.float64)
    return np.moveaxis((codes * scale).reshape(v.shape), -1, axis)


WIDE = False


def mx_kscale(k):
    if not WIDE:
        return np.ones(k)
    levels = np.array([10, -10, 5, -5, 0])
    if k % 512:
        return np.exp2(np.random.permutation(np.resize(levels, k // 32))).repeat(32)
    a = np.empty((k // 512, 16))
    for p in range(k // 512):
        a[p, :8] = np.random.permutation(np.resize(levels, 8))
        for g in range(8):
            far = levels[np.abs(levels - a[p, g]) >= 10]
            a[p, g + 8] = far[np.random.randint(len(far))]
    return np.exp2(a.ravel()).repeat(32)


def f64(x):
    return np.asarray(x).astype(np.float64)


def striped(idx):
    return np.tile(idx.reshape(-1, 16).T, (8, 1)).astype(np.uint16)


def unstriped(offs):
    return offs[:16].T.reshape(-1).astype(np.int64)


def striped8(idx):
    return np.concatenate([x.reshape(-1, 16).T for x in idx]).astype(np.uint16)


def runs(offs, k):
    lists = np.stack([offs[16 * r : 16 * r + 16].T.reshape(-1) for r in range(8)]).astype(np.int64)
    return lists[np.arange(k) % 512 // 64]


def pack_weight(w):
    k, n = w.shape
    w = f64(np.asarray(w, np.float32).astype(ml_dtypes.bfloat16)).reshape(k // 32, 32, n)
    amax = np.abs(w).max(1)
    byte = np.clip(np.where(amax > 0, np.frexp(amax)[1] - 1 + 127 - 7, 1), 1, 254)
    scaled = (w * np.exp2(127.0 - byte)[:, None, :]).reshape(k, n).astype(np.float32)
    words = np.ascontiguousarray(scaled.reshape(k // 512, 128, 4, n).transpose(0, 1, 3, 2)).astype(ml_dtypes.float8_e4m3fn).view(np.uint8)
    return words, np.ascontiguousarray(byte.astype(np.uint8).reshape(k // 512, 16, n))


def unpack_weight(words, scales):
    g, p, n, _ = words.shape
    vals = np.ascontiguousarray(words).view(ml_dtypes.float8_e4m3fn).astype(np.float64) * np.repeat(np.exp2(scales.astype(np.float64) - 127.0), 8, axis=1)[..., None]
    return vals.transpose(0, 1, 3, 2).reshape(g * 512, n)

def planes(y):
    n, m = y.shape
    v = y.astype(np.float32).astype(ml_dtypes.bfloat16).astype(np.float64).reshape(n // 32, 32, m)
    top = np.abs(v).max(1)
    byte = np.clip(np.where(top > 0, np.frexp(top)[1] - 1 + 127 - 7, 1), 1, 254)
    codes = (v * np.exp2(127.0 - byte)[:, None, :]).reshape(n, m).astype(np.float32).astype(ml_dtypes.float8_e4m3fn).view(np.uint8)
    words = codes.reshape(n // 512, 128, 4, m).transpose(0, 1, 3, 2)
    return np.ascontiguousarray(words), np.ascontiguousarray(byte.astype(np.uint8).reshape(n // 512, 16, m))


K, T, S, N, H = 512, 2048, 512, 512, 512


def setup_inputs():
    n = np.random.standard_normal
    s = mx_kscale(K)[:, None]
    u = mx_kscale(S)
    packed_xT = pack_weight(n((K, T)) * s)
    return {
        "x_words": packed_xT[0],
        "x_scales": packed_xT[1],
        "wa": (n((K, H)) / np.sqrt(K) / s).astype(np.float32),
        "wb": (n((K, N)) / np.sqrt(K) / s).astype(np.float32),
        "gt": (np.random.uniform(0.5, 1.5, (S, 1)) * u[:, None]).astype(np.float32),
        "gi": (np.random.uniform(0.5, 1.5, (S, 1)) / u[:, None]).astype(np.float32),
        "offs": striped(np.random.permutation(T)[:S]),
        "two": striped(np.random.permutation(T)[:S]),
        "n1": striped8(np.stack([np.random.permutation(H) for _ in range(8)])),
        "n2": striped8(np.stack([np.random.permutation(H) for _ in range(8)])),
        "n3": striped8(np.stack([np.random.permutation(H) for _ in range(8)])),
        "n4": striped8(np.stack([np.random.permutation(N) for _ in range(8)])),
        "n5": striped8(np.stack([np.random.permutation(N) for _ in range(8)])),
    }


def reference(x_words, x_scales, wa, wb, gt, gi, offs, two, n1, n2, n3, n4, n5):
    xq = unpack_weight(x_words, x_scales)[:, unstriped(offs)]
    a = xq.T @ mxq(f64(wa), 0, "e4m3")
    b1 = a[np.arange(S)[:, None], runs(n1, S)]
    b2 = a[np.arange(S)[:, None], runs(n2, S)]
    b3 = a[np.arange(S)[:, None], runs(n3, S)]
    z = f64(gt) * (np.maximum(np.maximum(b1, b2), b3) - (0.5 * (np.maximum(np.minimum(b1, b2), np.minimum(np.maximum(b1, b2), b3)))))
    x_two = unpack_weight(x_words, x_scales)[:, unstriped(two)]
    b = x_two.T @ mxq(f64(wb), 0, "e4m3")
    z2 = f64(gi) * b
    cv = 0.0625 * ((mxq(z, 0, "e4m3").T @ mxq(z2, 0, "e4m3")))
    ex = np.exp(cv)
    out_0 = np.log(ex + ex[np.arange(H)[:, None], runs(n4, H)]) - (cv[np.arange(H)[:, None], runs(n5, H)])
    return (out_0,) + planes(out_0)

@@ -1,0 +1,303 @@
+from contextlib import ExitStack
+
+import concourse.mybir as mybir
+from concourse.masks import make_identity
+
+K, T, S, H, N = 512, 2048, 512, 512, 512
+FLOPS = 2 * S * K * H + 2 * S * K * N + 2 * H * S * N
+
+F32 = mybir.dt.float32
+BF16 = mybir.dt.bfloat16
+I32 = mybir.dt.int32
+U32 = mybir.dt.uint32
+U16 = mybir.dt.uint16
+U8 = mybir.dt.uint8
+FP8X4 = mybir.dt.float8_e4m3fn_x4
+ALU = mybir.AluOpType
+ACT = mybir.ActivationFunctionType
+
+P = 128
+PACK = 4
+HALF = 256
+PER_COL = 16
+
+
+def tile_picked_momtop2lse_none_po_kernel(
+    tc, x_words, x_scales, wa, wb, gt, gi, offs, two, n1, n2, n3, n4, n5, out_0, out_1, out_2
+):
+    nc = tc.nc
+    with ExitStack() as ctx:
+        lists = ctx.enter_context(tc.tile_pool(name="lists", bufs=1))
+        keep = ctx.enter_context(tc.tile_pool(name="keep", bufs=1))
+        psum = ctx.enter_context(tc.psum_pool(name="psum", bufs=1))
+
+        def sb(name, shape, dtype):
+            return keep.tile(shape, dtype, name=name, align_bytes=64)
+
+        def bank(b, name):
+            return psum.tile([P, 512], F32, name=name, tag="bank%d" % b)
+
+        def load_list(name, src):
+            tile = lists.tile([P, S // PER_COL], U16, name=name)
+            nc.sync.dma_start(tile[:], src)
+            return tile
+
+        def cols_of(tile, c0, c1):
+            return tile[:, c0 // PER_COL : c1 // PER_COL]
+
+        xs = sb("xs", [P, T], U8)
+        nc.vector.memset(xs[:].bitcast(I32), 0)
+        offs_sb = load_list("offs_sb", offs)
+        xw = sb("xw", [P, T], I32)
+        nc.sync.dma_start(xw[:], x_words[0].rearrange("p c r -> p (c r)").bitcast(I32))
+        for q in range(4):
+            nc.scalar.dma_start(
+                xs[32 * q : 32 * q + 4, :].bitcast(I32), x_scales[0, 4 * q : 4 * q + 4, :].bitcast(I32)
+            )
+        two_sb = load_list("two_sb", two)
+        wa_raw = []
+        for h in range(2):
+            raw = sb("wa_raw%d" % h, [P, PACK, HALF], F32)
+            nc.sync.dma_start(raw[:], wa.rearrange("(p j) c -> p j c", j=PACK)[:, :, h * HALF : (h + 1) * HALF])
+            wa_raw.append(raw)
+        n1_sb = load_list("n1_sb", n1)
+        n2_sb = load_list("n2_sb", n2)
+        n3_sb = load_list("n3_sb", n3)
+        wb_raw = sb("wb_raw", [P, PACK, N], F32)
+        nc.sync.dma_start(wb_raw[:], wb.rearrange("(p j) c -> p j c", j=PACK))
+        n4_sb = load_list("n4_sb", n4)
+        n5_sb = load_list("n5_sb", n5)
+
+        g_rows = sb("g_rows", [P, P], F32)
+        nc.vector.memset(g_rows[:], 0.0)
+        for r, src in ((0, gt), (PACK, gi)):
+            nc.scalar.dma_start(
+                g_rows[r : r + PACK, :].rearrange("t (b e) -> t b e", e=8),
+                src.rearrange("(b t e) o -> t b (e o)", t=PACK, e=8),
+            )
+        ident = sb("ident", [P, P], F32)
+        make_identity(nc, ident[:])
+        g_ps = bank(7, "g_ps")
+        nc.tensor.transpose(g_ps[:, 0:P], g_rows[:], ident[:])
+        g_cols = sb("g_cols", [P, 2 * PACK], F32)
+        nc.scalar.copy(g_cols[:], g_ps[:, 0 : 2 * PACK])
+        gt_abs = sb("gt_abs", [P, PACK], F32)
+        nc.scalar.activation(gt_abs[:], g_cols[:, 0:PACK], ACT.Abs)
+        gt_step = sb("gt_step", [P, PACK], F32)
+        nc.vector.tensor_scalar(gt_step[:], g_cols[:, 0:PACK], 0.0, 2.0, ALU.is_ge, ALU.mult)
+        gi_signed = sb("gi_signed", [P, PACK], F32)
+        nc.vector.scalar_tensor_tensor(gi_signed[:], gt_step[:], -1.0, g_cols[:, PACK:], ALU.add, ALU.mult)
+
+        def gather_words(name, lst):
+            words = sb(name, [P, S], U32)
+            nc.vector.tensor_copy(
+                words[:].rearrange("p (t b e) -> p b t e", t=PACK, e=8), xw[:].bitcast(U32).indirect(lst[:])
+            )
+            return words
+
+        def gather_scales(name, lst):
+            listed = sb(name + "_listed", [P, S], U8)
+            nc.vector.tensor_copy(listed[:], xs[:].indirect(lst[:]))
+            return listed
+
+        def deal_scales(name, listed):
+            dealt = sb(name, [P, S], U8)
+            nc.vector.tensor_copy(
+                dealt[:].bitcast(I32).rearrange("p (t b e) -> p t b e", t=PACK, e=2),
+                listed[:].bitcast(I32).rearrange("p (b t e) -> p t b e", t=PACK, e=2),
+            )
+            return dealt
+
+        def interleave(engine_copy, dst, src):
+            engine_copy(
+                dst.rearrange("p (c i) t -> p c t i", i=4), src.rearrange("p t (c i) -> p c t i", i=4)
+            )
+
+        def quantize(codes, scales, grouped, c0, c1):
+            nc.vector.quantize_mx(
+                out=codes[:, c0:c1].bitcast(FP8X4),
+                scales=scales[:, c0:c1],
+                in_=grouped[:, c0:c1, :].rearrange("p c t -> p (c t)"),
+            )
+
+        def product(acc, l_codes, l_scales, t, r_codes, r_scales):
+            nc.tensor.matmul_mx(
+                out=acc[:],
+                lhsT=l_codes[:, t * P : (t + 1) * P].bitcast(FP8X4),
+                lhsT_scale=l_scales[:, t * P : (t + 1) * P],
+                rhs=r_codes[:].bitcast(FP8X4),
+                rhs_scale=r_scales[:],
+                start=True,
+                stop=True,
+            )
+
+        xa_words = gather_words("xa_words", offs_sb)
+        xa_listed = gather_scales("xa_scales", offs_sb)
+        wa_bf = sb("wa_bf", [P, H, PACK], BF16)
+        for h in range(2):
+            interleave(nc.scalar.copy, wa_bf[:, h * HALF : (h + 1) * HALF, :], wa_raw[h][:])
+        xb_words = gather_words("xb_words", two_sb)
+        xa_scales = deal_scales("xa_scales", xa_listed)
+        wa_codes = sb("wa_codes", [P, H], U32)
+        wa_scales = sb("wa_scales", [P, H], U8)
+        quantize(wa_codes, wa_scales, wa_bf, 0, H)
+        xb_listed = gather_scales("xb_scales", two_sb)
+        a_win = []
+        for t in range(PACK):
+            acc = bank(t, "a_ps%d" % t)
+            product(acc, xa_words, xa_scales, t, wa_codes, wa_scales)
+            win = sb("a_win%d" % t, [P, H], F32)
+            nc.scalar.activation(win[:], acc[:], ACT.Copy, scale=gt_abs[:, t : t + 1])
+            a_win.append(win)
+        xb_scales = deal_scales("xb_scales", xb_listed)
+
+        wb_bf = sb("wb_bf", [P, N, PACK], BF16)
+        interleave(nc.scalar.copy, wb_bf[:], wb_raw[:])
+
+        stage = []
+        for h in range(2):
+            stage.append({nm: sb("%s%d" % (nm, h), [P, PACK, HALF], F32) for nm in ("b1", "d", "gap", "hi", "up", "k", "m", "z")})
+        z_bf = sb("z_bf", [P, H, PACK], BF16)
+
+        def look(h, t, lst):
+            return a_win[t][:].indirect(cols_of(lst, h * HALF, (h + 1) * HALF))
+
+        def g1(h, t):
+            nc.vector.tensor_copy(stage[h]["b1"][:, t, :], look(h, t, n1_sb))
+
+        def g2(h, t):
+            nc.vector.tensor_tensor(stage[h]["d"][:, t, :], look(h, t, n2_sb), stage[h]["b1"][:, t, :], ALU.subtract)
+
+        def g3(h, t):
+            nc.vector.tensor_tensor(stage[h]["up"][:, t, :], look(h, t, n3_sb), stage[h]["hi"][:, t, :], ALU.subtract)
+
+        def flat(h, nm, ts):
+            return stage[h][nm][:, ts, :].rearrange("p t c -> p (t c)")
+
+        def op_gap(h, ts):
+            nc.scalar.activation(flat(h, "gap", ts), flat(h, "d", ts), ACT.Abs, scale=0.5)
+
+        def op_hi(h, ts):
+            nc.vector.scalar_tensor_tensor(flat(h, "hi", ts), flat(h, "d", ts), 0.0, flat(h, "b1", ts), ALU.max, ALU.add)
+
+        def op_k(h, ts):
+            nc.vector.scalar_tensor_tensor(flat(h, "k", ts), flat(h, "up", ts), -0.5, flat(h, "gap", ts), ALU.mult, ALU.min)
+
+        def op_m(h, ts):
+            nc.vector.tensor_tensor(flat(h, "m", ts), flat(h, "up", ts), flat(h, "k", ts), ALU.max)
+
+        def op_z(h, ts):
+            nc.vector.scalar_tensor_tensor(flat(h, "z", ts), flat(h, "hi", ts), 0.5, flat(h, "m", ts), ALU.mult, ALU.add)
+
+        def deal_z(engine_copy, h, c0, c1):
+            m0, m1 = (h * HALF + c0) // PACK, (h * HALF + c1) // PACK
+            engine_copy(
+                z_bf[:].rearrange("p (u m) t -> p m t u", u=PACK)[:, m0:m1, :, :],
+                stage[h]["z"][:, :, c0:c1].rearrange("p t (m u) -> p m t u", u=PACK),
+            )
+
+        pairs = (slice(0, 2), slice(2, 4))
+        every = slice(0, 4)
+
+        for t in range(PACK):
+            g1(0, t)
+        for t in range(PACK):
+            g2(0, t)
+        op_gap(0, every)
+        g1(1, 0)
+        op_hi(0, every)
+        g1(1, 1)
+        for t in range(PACK):
+            g3(0, t)
+
+        wb_codes = sb("wb_codes", [P, N], U32)
+        wb_scales = sb("wb_scales", [P, N], U8)
+        quantize(wb_codes, wb_scales, wb_bf, 0, N)
+        z2_rows = sb("z2_rows", [P, PACK, N], BF16)
+        for t in range(PACK):
+            acc = bank(PACK + t, "b_ps%d" % t)
+            product(acc, xb_words, xb_scales, t, wb_codes, wb_scales)
+            nc.scalar.activation(z2_rows[:, t, :], acc[:], ACT.Copy, scale=gi_signed[:, t : t + 1])
+        z2_bf = sb("z2_bf", [P, N, PACK], BF16)
+        interleave(nc.scalar.copy, z2_bf[:], z2_rows[:])
+
+        op_k(0, every)
+        g1(1, 2)
+        op_m(0, every)
+        g1(1, 3)
+        op_z(0, every)
+        for t in range(PACK):
+            g2(1, t)
+        for ts in pairs:
+            op_gap(1, ts)
+        deal_z(nc.scalar.copy, 0, 0, HALF)
+        for ts in pairs:
+            op_hi(1, ts)
+        for t in range(PACK):
+            g3(1, t)
+        z2_codes = sb("z2_codes", [P, N], U32)
+        z2_scales = sb("z2_scales", [P, N], U8)
+        quantize(z2_codes, z2_scales, z2_bf, 0, N)
+        for op in (op_k, op_m, op_z):
+            for ts in pairs:
+                op(1, ts)
+        deal_z(nc.scalar.copy, 1, 0, 96)
+        deal_z(nc.vector.tensor_copy, 1, 96, HALF)
+
+        z_codes = sb("z_codes", [P, H], U32)
+        z_scales = sb("z_scales", [P, H], U8)
+        cv_ps = []
+        for u in range(PACK):
+            quantize(z_codes, z_scales, z_bf, u * P, (u + 1) * P)
+        for u in range(PACK):
+            acc = bank(u, "cv_ps%d" % u)
+            product(acc, z_codes, z_scales, u, z2_codes, z2_scales)
+            cv_ps.append(acc)
+
+        ex = sb("ex", [P, PACK, N], F32)
+        both = sb("both", [P, PACK, N], F32)
+        logs = sb("logs", [P, PACK, N], F32)
+        res = sb("res", [P, PACK, N], F32)
+        ex_win = [sb("ex_win%d" % u, [P, 2 * N], F32) for u in range(PACK)]
+        neg_win = [sb("neg_win%d" % u, [P, 2 * N], F32) for u in range(PACK)]
+
+        def neg_copy(u):
+            nc.vector.tensor_scalar(neg_win[u][:, 0:N], cv_ps[u][:], -0.0625, None, ALU.mult)
+
+        neg_copy(1)
+        neg_copy(2)
+        for u in range(PACK):
+            nc.scalar.activation(ex_win[u][:, 0:N], cv_ps[u][:], ACT.Exp, scale=0.0625)
+            nc.scalar.activation(ex[:, u, :], cv_ps[u][:], ACT.Exp, scale=0.0625)
+            nc.vector.tensor_tensor(both[:, u, :], ex_win[u][:].indirect(n4_sb[:]), ex[:, u, :], ALU.add)
+        neg_copy(0)
+        neg_copy(3)
+        for u in range(PACK):
+            nc.scalar.activation(logs[:, u, :], both[:, u, :], ACT.Ln)
+
+        out_rows = out_0.rearrange("(p u) c -> p u c", u=PACK)
+        res_bf = sb("res_bf", [P, N, PACK], BF16)
+        o_codes = sb("o_codes", [P, N], U32)
+        o_scales = sb("o_scales", [P, N], U8)
+        words_out = out_1[0].rearrange("p c r -> p (c r)").bitcast(I32)
+
+        def finish(u, c0, c1):
+            nc.vector.tensor_tensor(
+                res[:, u, c0:c1], neg_win[u][:].indirect(cols_of(n5_sb, c0, c1)), logs[:, u, c0:c1], ALU.add
+            )
+            nc.sync.dma_start(out_rows[:, u, c0:c1], res[:, u, c0:c1])
+
+        for u in range(PACK - 1):
+            finish(u, 0, N)
+        finish(PACK - 1, 0, HALF)
+        interleave(nc.scalar.copy, res_bf[:, 0:HALF, :], res[:, :, 0:HALF])
+        finish(PACK - 1, HALF, N)
+        interleave(nc.vector.tensor_copy, res_bf[:, HALF:N, :], res[:, :, HALF:N])
+        for h in range(2):
+            quantize(o_codes, o_scales, res_bf, h * HALF, (h + 1) * HALF)
+            nc.sync.dma_start(words_out[:, h * HALF : (h + 1) * HALF], o_codes[:, h * HALF : (h + 1) * HALF].bitcast(I32))
+        for q in range(4):
+            queue = nc.scalar if q % 2 else nc.sync
+            queue.dma_start(
+                out_2[0, 4 * q : 4 * q + 4, :].bitcast(I32), o_scales[32 * q : 32 * q + 4, :].bitcast(I32)
+            )

@@ -31,8 +31,8 @@ def tile_picked_momtop2lse_none_po_kernel(
         keep = ctx.enter_context(tc.tile_pool(name="keep", bufs=1))
         psum = ctx.enter_context(tc.psum_pool(name="psum", bufs=1))
 
-        def sb(name, shape, dtype):
-            return keep.tile(shape, dtype, name=name, align_bytes=64)
+        def sb(name, shape, dtype, tag=None):
+            return keep.tile(shape, dtype, name=name, tag=tag or name, align_bytes=64)
 
         def bank(b, name):
             return psum.tile([P, 512], F32, name=name, tag="bank%d" % b)
@@ -46,20 +46,27 @@ def tile_picked_momtop2lse_none_po_kernel(
             return tile[:, c0 // PER_COL : c1 // PER_COL]
 
         xs = sb("xs", [P, T], U8)
-        nc.vector.memset(xs[:].bitcast(I32), 0)
+        nc.gpsimd.memset(xs[:].bitcast(I32), 0)
         offs_sb = load_list("offs_sb", offs)
-        xw = sb("xw", [P, T], I32)
-        nc.sync.dma_start(xw[:], x_words[0].rearrange("p c r -> p (c r)").bitcast(I32))
         for q in range(4):
-            nc.scalar.dma_start(
+            nc.sync.dma_start(
                 xs[32 * q : 32 * q + 4, :].bitcast(I32), x_scales[0, 4 * q : 4 * q + 4, :].bitcast(I32)
             )
-        two_sb = load_list("two_sb", two)
         wa_raw = []
         for h in range(2):
             raw = sb("wa_raw%d" % h, [P, PACK, HALF], F32)
             nc.sync.dma_start(raw[:], wa.rearrange("(p j) c -> p j c", j=PACK)[:, :, h * HALF : (h + 1) * HALF])
             wa_raw.append(raw)
+        xw = sb("xw", [P, T], I32)
+        nc.sync.dma_start(xw[:], x_words[0].rearrange("p c r -> p (c r)").bitcast(I32))
+        g_rows = sb("g_rows", [P, P], F32)
+        nc.vector.memset(g_rows[:], 0.0)
+        for r, src in ((0, gt), (PACK, gi)):
+            nc.sync.dma_start(
+                g_rows[r : r + PACK, :].rearrange("t (b e) -> t b e", e=8),
+                src.rearrange("(b t e) o -> t b (e o)", t=PACK, e=8),
+            )
+        two_sb = load_list("two_sb", two)
         n1_sb = load_list("n1_sb", n1)
         n2_sb = load_list("n2_sb", n2)
         n3_sb = load_list("n3_sb", n3)
@@ -68,26 +75,8 @@ def tile_picked_momtop2lse_none_po_kernel(
         n4_sb = load_list("n4_sb", n4)
         n5_sb = load_list("n5_sb", n5)
 
-        g_rows = sb("g_rows", [P, P], F32)
-        nc.vector.memset(g_rows[:], 0.0)
-        for r, src in ((0, gt), (PACK, gi)):
-            nc.scalar.dma_start(
-                g_rows[r : r + PACK, :].rearrange("t (b e) -> t b e", e=8),
-                src.rearrange("(b t e) o -> t b (e o)", t=PACK, e=8),
-            )
         ident = sb("ident", [P, P], F32)
         make_identity(nc, ident[:])
-        g_ps = bank(7, "g_ps")
-        nc.tensor.transpose(g_ps[:, 0:P], g_rows[:], ident[:])
-        g_cols = sb("g_cols", [P, 2 * PACK], F32)
-        nc.scalar.copy(g_cols[:], g_ps[:, 0 : 2 * PACK])
-        gt_abs = sb("gt_abs", [P, PACK], F32)
-        nc.scalar.activation(gt_abs[:], g_cols[:, 0:PACK], ACT.Abs)
-        gt_step = sb("gt_step", [P, PACK], F32)
-        nc.vector.tensor_scalar(gt_step[:], g_cols[:, 0:PACK], 0.0, 2.0, ALU.is_ge, ALU.mult)
-        gi_signed = sb("gi_signed", [P, PACK], F32)
-        nc.vector.scalar_tensor_tensor(gi_signed[:], gt_step[:], -1.0, g_cols[:, PACK:], ALU.add, ALU.mult)
-
         def gather_words(name, lst):
             words = sb(name, [P, S], U32)
             nc.vector.tensor_copy(
@@ -113,6 +102,9 @@ def tile_picked_momtop2lse_none_po_kernel(
                 dst.rearrange("p (c i) t -> p c t i", i=4), src.rearrange("p t (c i) -> p c t i", i=4)
             )
 
+        def negate(dst, src):
+            nc.scalar.activation(dst, src, ACT.Copy, scale=-1.0)
+
         def quantize(codes, scales, grouped, c0, c1):
             nc.vector.quantize_mx(
                 out=codes[:, c0:c1].bitcast(FP8X4),
@@ -131,118 +123,152 @@ def tile_picked_momtop2lse_none_po_kernel(
                 stop=True,
             )
 
-        xa_words = gather_words("xa_words", offs_sb)
         xa_listed = gather_scales("xa_scales", offs_sb)
-        wa_bf = sb("wa_bf", [P, H, PACK], BF16)
-        for h in range(2):
-            interleave(nc.scalar.copy, wa_bf[:, h * HALF : (h + 1) * HALF, :], wa_raw[h][:])
-        xb_words = gather_words("xb_words", two_sb)
         xa_scales = deal_scales("xa_scales", xa_listed)
+        wa_bf = sb("wa_bf", [P, H, PACK], BF16)
         wa_codes = sb("wa_codes", [P, H], U32)
         wa_scales = sb("wa_scales", [P, H], U8)
-        quantize(wa_codes, wa_scales, wa_bf, 0, H)
+        for h in range(2):
+            interleave(negate, wa_bf[:, h * HALF : (h + 1) * HALF, :], wa_raw[h][:])
+            quantize(wa_codes, wa_scales, wa_bf, h * HALF, (h + 1) * HALF)
+        g_ps = bank(0, "g_ps")
+        nc.tensor.transpose(g_ps[:, 0:P], g_rows[:], ident[:])
+        g_cols = sb("g_cols", [P, 2 * PACK], F32, tag="wa_raw1")
+        nc.scalar.copy(g_cols[:], g_ps[:, 0 : 2 * PACK])
+        gt_abs = sb("gt_abs", [P, PACK], F32, tag="turns")
+        nc.scalar.activation(gt_abs[:], g_cols[:, 0:PACK], ACT.Abs)
+
+        xa_words = gather_words("xa_words", offs_sb)
+        xb_words = gather_words("xb_words", two_sb)
         xb_listed = gather_scales("xb_scales", two_sb)
+        xb_scales = deal_scales("xb_scales", xb_listed)
+        gt_step = sb("gt_step", [P, PACK], F32, tag="xb_scales_listed")
+        nc.vector.tensor_scalar(gt_step[:], g_cols[:, 0:PACK], 0.0, 2.0, ALU.is_ge, ALU.mult)
+        gi_signed = sb("gi_signed", [P, PACK], F32)
+        nc.vector.scalar_tensor_tensor(gi_signed[:], gt_step[:], -1.0, g_cols[:, PACK:], ALU.add, ALU.mult)
         a_win = []
         for t in range(PACK):
             acc = bank(t, "a_ps%d" % t)
             product(acc, xa_words, xa_scales, t, wa_codes, wa_scales)
-            win = sb("a_win%d" % t, [P, H], F32)
-            nc.scalar.activation(win[:], acc[:], ACT.Copy, scale=gt_abs[:, t : t + 1])
+            win = sb("a_win%d" % t, [P, 2 * H], F32)
+            nc.scalar.activation(win[:, 0:H], acc[:], ACT.Copy, scale=gt_abs[:, t : t + 1])
             a_win.append(win)
-        xb_scales = deal_scales("xb_scales", xb_listed)
 
-        wb_bf = sb("wb_bf", [P, N, PACK], BF16)
+        wb_bf = sb("wb_bf", [P, N, PACK], BF16, tag="turns")
         interleave(nc.scalar.copy, wb_bf[:], wb_raw[:])
 
-        stage = []
-        for h in range(2):
-            stage.append({nm: sb("%s%d" % (nm, h), [P, PACK, HALF], F32) for nm in ("b1", "d", "gap", "hi", "up", "k", "m", "z")})
+        c1 = sb("c1", [P, PACK, H], F32)
         z_bf = sb("z_bf", [P, H, PACK], BF16)
+        z_dealt = z_bf[:].rearrange("p (u m) t -> p m t u", u=PACK)
 
-        def look(h, t, lst):
-            return a_win[t][:].indirect(cols_of(lst, h * HALF, (h + 1) * HALF))
+        def look(t, lst, c0, c1):
+            return a_win[t][:].indirect(cols_of(lst, c0, c1))
 
-        def g1(h, t):
-            nc.vector.tensor_copy(stage[h]["b1"][:, t, :], look(h, t, n1_sb))
+        def turn(acc, terms, col0):
+            slots = acc[:].rearrange("p (t c) -> p t c", t=PACK)
+            for i, term in enumerate(terms):
+                for t in range(PACK):
+                    nc.tensor.matmul(
+                        slots[:, t, :],
+                        term[:, t, col0 : col0 + P],
+                        ident[:],
+                        start=(i == 0 and t == 0),
+                        stop=(i == len(terms) - 1 and t == PACK - 1),
+                        is_transpose=True,
+                    )
 
-        def g2(h, t):
-            nc.vector.tensor_tensor(stage[h]["d"][:, t, :], look(h, t, n2_sb), stage[h]["b1"][:, t, :], ALU.subtract)
+        def block(name, tag=None):
+            return sb(name, [P, PACK, P], F32, tag=tag)
 
-        def g3(h, t):
-            nc.vector.tensor_tensor(stage[h]["up"][:, t, :], look(h, t, n3_sb), stage[h]["hi"][:, t, :], ALU.subtract)
+        def by_tile(row):
+            return row.rearrange("p (t c) -> p t c", t=PACK)
 
-        def flat(h, nm, ts):
-            return stage[h][nm][:, ts, :].rearrange("p t c -> p (t c)")
-
-        def op_gap(h, ts):
-            nc.scalar.activation(flat(h, "gap", ts), flat(h, "d", ts), ACT.Abs, scale=0.5)
-
-        def op_hi(h, ts):
-            nc.vector.scalar_tensor_tensor(flat(h, "hi", ts), flat(h, "d", ts), 0.0, flat(h, "b1", ts), ALU.max, ALU.add)
-
-        def op_k(h, ts):
-            nc.vector.scalar_tensor_tensor(flat(h, "k", ts), flat(h, "up", ts), -0.5, flat(h, "gap", ts), ALU.mult, ALU.min)
-
-        def op_m(h, ts):
-            nc.vector.tensor_tensor(flat(h, "m", ts), flat(h, "up", ts), flat(h, "k", ts), ALU.max)
-
-        def op_z(h, ts):
-            nc.vector.scalar_tensor_tensor(flat(h, "z", ts), flat(h, "hi", ts), 0.5, flat(h, "m", ts), ALU.mult, ALU.add)
-
-        def deal_z(engine_copy, h, c0, c1):
-            m0, m1 = (h * HALF + c0) // PACK, (h * HALF + c1) // PACK
-            engine_copy(
-                z_bf[:].rearrange("p (u m) t -> p m t u", u=PACK)[:, m0:m1, :, :],
-                stage[h]["z"][:, :, c0:c1].rearrange("p t (m u) -> p m t u", u=PACK),
-            )
-
-        pairs = (slice(0, 2), slice(2, 4))
-        every = slice(0, 4)
+        def flat(tile):
+            return tile[:].rearrange("p t c -> p (t c)")
 
         for t in range(PACK):
-            g1(0, t)
-        for t in range(PACK):
-            g2(0, t)
-        op_gap(0, every)
-        g1(1, 0)
-        op_hi(0, every)
-        g1(1, 1)
-        for t in range(PACK):
-            g3(0, t)
+            nc.vector.tensor_copy(c1[:, t, :], look(t, n1_sb, 0, H))
 
         wb_codes = sb("wb_codes", [P, N], U32)
         wb_scales = sb("wb_scales", [P, N], U8)
         quantize(wb_codes, wb_scales, wb_bf, 0, N)
-        z2_rows = sb("z2_rows", [P, PACK, N], BF16)
+        diffs = sb("diffs", [P, PACK, H + HALF], F32, tag="turns")
+        dc, ec = diffs[:, :, 0:H], diffs[:, :, H:]
+        for t in range(PACK):
+            nc.vector.tensor_tensor(dc[:, t, :], look(t, n2_sb, 0, H), c1[:, t, :], ALU.subtract)
+
+        half_b1 = sb("half_b1", [P, 2, N], F32, tag="wb_raw")
+        for j in range(2):
+            acc = bank(j, "c1_ps%d" % j)
+            turn(acc, [c1], j * P)
+            nc.scalar.activation(half_b1[:, j, :], acc[:], ACT.Copy, scale=-0.5)
+
+        shared = sb("shared", [P, PACK, 2 * N], F32)
+        z2_rows = shared[:, :, HALF : HALF + N]
         for t in range(PACK):
             acc = bank(PACK + t, "b_ps%d" % t)
             product(acc, xb_words, xb_scales, t, wb_codes, wb_scales)
             nc.scalar.activation(z2_rows[:, t, :], acc[:], ACT.Copy, scale=gi_signed[:, t : t + 1])
         z2_bf = sb("z2_bf", [P, N, PACK], BF16)
-        interleave(nc.scalar.copy, z2_bf[:], z2_rows[:])
+        interleave(nc.scalar.copy, z2_bf[:], z2_rows)
 
-        op_k(0, every)
-        g1(1, 2)
-        op_m(0, every)
-        g1(1, 3)
-        op_z(0, every)
+        rise = shared[:, 0, :].rearrange("p (t c) -> p t c", t=PACK)
+        gap = shared[:, 1, :].rearrange("p (t c) -> p t c", t=PACK)
+        gap_t = [shared[:, 2 + j, 0:N] for j in range(2)]
+        half_rise = [shared[:, 2 + j, N:] for j in range(2)]
+        nc.scalar.activation(rise, dc[:, :, 0:HALF], ACT.Relu, scale=-1.0)
+        for j in range(2):
+            acc = bank(2 + j, "dc_ps%d" % j)
+            turn(acc, [dc], j * P)
+            nc.scalar.activation(gap_t[j], acc[:], ACT.Abs, scale=0.5)
+            nc.scalar.activation(half_rise[j], acc[:], ACT.Relu, scale=-0.5)
+        nc.scalar.activation(gap, dc[:, :, HALF:H], ACT.Abs, scale=0.5)
+
         for t in range(PACK):
-            g2(1, t)
-        for ts in pairs:
-            op_gap(1, ts)
-        deal_z(nc.scalar.copy, 0, 0, HALF)
-        for ts in pairs:
-            op_hi(1, ts)
+            nc.vector.tensor_tensor(ec[:, t, :], look(t, n3_sb, 0, HALF), c1[:, t, 0:HALF], ALU.subtract)
+        lo = sb("lo", [P, PACK, HALF], F32)
+        nc.vector.scalar_tensor_tensor(lo[:], dc[:, :, HALF:H], 0.0, c1[:, :, HALF:H], ALU.min, ALU.add)
+        over = sb("over", [P, PACK, HALF], F32)
         for t in range(PACK):
-            g3(1, t)
+            nc.vector.tensor_tensor(over[:, t, :], look(t, n3_sb, HALF, H), lo[:, t, :], ALU.subtract)
+
+        over_ps, low_t, top_t = [], [], []
+        for j in range(2):
+            over_ps.append(bank(PACK + j, "over_ps%d" % j))
+            turn(over_ps[j], [ec, rise], j * P)
+        for j in range(2):
+            low_t.append(block("low_t%d" % j))
+            nc.vector.scalar_tensor_tensor(flat(low_t[j]), over_ps[j][:], 0.5, gap_t[j], ALU.mult, ALU.min)
+        for j in range(2):
+            top_t.append(block("top_t%d" % j))
+            nc.vector.scalar_tensor_tensor(flat(top_t[j]), over_ps[j][:], -1.0, flat(low_t[j]), ALU.mult, ALU.max)
+        for j in range(2):
+            acc = bank(6 + j, "z_ps%d" % j)
+            turn(acc, [by_tile(half_b1[:, j, :]), by_tile(half_rise[j]), top_t[j]], 0)
+            nc.scalar.copy(
+                z_dealt[:, 32 * j : 32 * j + 32, :, :], acc[:].rearrange("p (t m u) -> p m t u", t=PACK, u=PACK)
+            )
+
+        low, top, z = [], [], []
+        for j in range(2):
+            low.append(block("low%d" % j, tag="low_t%d" % j))
+            cs = slice(j * P, (j + 1) * P)
+            nc.vector.scalar_tensor_tensor(low[j][:], over[:, :, cs], 0.5, gap[:, :, cs], ALU.mult, ALU.min)
+        for j in range(2):
+            top.append(block("top%d" % j))
+            cs = slice(j * P, (j + 1) * P)
+            nc.vector.scalar_tensor_tensor(top[j][:], over[:, :, cs], -1.0, low[j][:], ALU.mult, ALU.max)
         z2_codes = sb("z2_codes", [P, N], U32)
         z2_scales = sb("z2_scales", [P, N], U8)
         quantize(z2_codes, z2_scales, z2_bf, 0, N)
-        for op in (op_k, op_m, op_z):
-            for ts in pairs:
-                op(1, ts)
-        deal_z(nc.scalar.copy, 1, 0, 96)
-        deal_z(nc.vector.tensor_copy, 1, 96, HALF)
+        for j, engine_copy in enumerate((nc.scalar.copy, nc.vector.tensor_copy)):
+            z.append(block("z%d" % j))
+            cs = slice(j * P, (j + 1) * P)
+            nc.vector.scalar_tensor_tensor(z[j][:], lo[:, :, cs], -0.5, top[j][:], ALU.mult, ALU.add)
+        for j, engine_copy in enumerate((nc.scalar.copy, nc.vector.tensor_copy)):
+            engine_copy(
+                z_dealt[:, 64 + 32 * j : 96 + 32 * j, :, :], z[j][:].rearrange("p t (m u) -> p m t u", u=PACK)
+            )
 
         z_codes = sb("z_codes", [P, H], U32)
         z_scales = sb("z_scales", [P, H], U8)
@@ -270,9 +296,9 @@ def tile_picked_momtop2lse_none_po_kernel(
             nc.scalar.activation(ex_win[u][:, 0:N], cv_ps[u][:], ACT.Exp, scale=0.0625)
             nc.scalar.activation(ex[:, u, :], cv_ps[u][:], ACT.Exp, scale=0.0625)
             nc.vector.tensor_tensor(both[:, u, :], ex_win[u][:].indirect(n4_sb[:]), ex[:, u, :], ALU.add)
-        neg_copy(0)
-        neg_copy(3)
-        for u in range(PACK):
+        for u in (1, 2, 0, 3):
+            if u in (0, 3):
+                nc.scalar.activation(neg_win[u][:, 0:N], cv_ps[u][:], ACT.Copy, scale=-0.0625)
             nc.scalar.activation(logs[:, u, :], both[:, u, :], ACT.Ln)
 
         out_rows = out_0.rearrange("(p u) c -> p u c", u=PACK)
@@ -287,15 +313,22 @@ def tile_picked_momtop2lse_none_po_kernel(
             )
             nc.sync.dma_start(out_rows[:, u, c0:c1], res[:, u, c0:c1])
 
-        for u in range(PACK - 1):
-            finish(u, 0, N)
-        finish(PACK - 1, 0, HALF)
+        def planes(c0, c1):
+            quantize(o_codes, o_scales, res_bf, c0, c1)
+            nc.sync.dma_start(words_out[:, c0:c1], o_codes[:, c0:c1].bitcast(I32))
+
+        finish(1, 0, N)
+        finish(2, 0, N)
+        finish(0, 0, HALF)
+        finish(3, 0, HALF)
         interleave(nc.scalar.copy, res_bf[:, 0:HALF, :], res[:, :, 0:HALF])
-        finish(PACK - 1, HALF, N)
-        interleave(nc.vector.tensor_copy, res_bf[:, HALF:N, :], res[:, :, HALF:N])
-        for h in range(2):
-            quantize(o_codes, o_scales, res_bf, h * HALF, (h + 1) * HALF)
-            nc.sync.dma_start(words_out[:, h * HALF : (h + 1) * HALF], o_codes[:, h * HALF : (h + 1) * HALF].bitcast(I32))
+        finish(0, HALF, N)
+        finish(3, HALF, N)
+        split = HALF + 80
+        interleave(nc.scalar.copy, res_bf[:, HALF:split, :], res[:, :, HALF:split])
+        interleave(nc.vector.tensor_copy, res_bf[:, split:N, :], res[:, :, split:N])
+        planes(0, HALF)
+        planes(HALF, N)
         for q in range(4):
             queue = nc.scalar if q % 2 else nc.sync
             queue.dma_start(

@@ -20,6 +20,7 @@ P = 128
 PACK = 4
 HALF = 256
 PER_COL = 16
+TURNED = 3
 
 
 def tile_picked_momtop2lse_none_po_kernel(
@@ -48,17 +49,17 @@ def tile_picked_momtop2lse_none_po_kernel(
         xs = sb("xs", [P, T], U8)
         nc.gpsimd.memset(xs[:].bitcast(I32), 0)
         offs_sb = load_list("offs_sb", offs)
+        two_sb = load_list("two_sb", two)
         for q in range(4):
             nc.sync.dma_start(
                 xs[32 * q : 32 * q + 4, :].bitcast(I32), x_scales[0, 4 * q : 4 * q + 4, :].bitcast(I32)
             )
-        wa_raw = []
-        for h in range(2):
-            raw = sb("wa_raw%d" % h, [P, PACK, HALF], F32)
-            nc.sync.dma_start(raw[:], wa.rearrange("(p j) c -> p j c", j=PACK)[:, :, h * HALF : (h + 1) * HALF])
-            wa_raw.append(raw)
+        wa_rows = wa.rearrange("(p j) c -> p j c", j=PACK)
+        wa_raw = [sb("wa_raw%d" % h, [P, PACK, HALF], F32) for h in range(2)]
+        nc.sync.dma_start(wa_raw[0][:], wa_rows[:, :, 0:HALF])
         xw = sb("xw", [P, T], I32)
         nc.sync.dma_start(xw[:], x_words[0].rearrange("p c r -> p (c r)").bitcast(I32))
+        nc.sync.dma_start(wa_raw[1][:], wa_rows[:, :, HALF:H])
         g_rows = sb("g_rows", [P, P], F32)
         nc.vector.memset(g_rows[:], 0.0)
         for r, src in ((0, gt), (PACK, gi)):
@@ -66,7 +67,6 @@ def tile_picked_momtop2lse_none_po_kernel(
                 g_rows[r : r + PACK, :].rearrange("t (b e) -> t b e", e=8),
                 src.rearrange("(b t e) o -> t b (e o)", t=PACK, e=8),
             )
-        two_sb = load_list("two_sb", two)
         n1_sb = load_list("n1_sb", n1)
         n2_sb = load_list("n2_sb", n2)
         n3_sb = load_list("n3_sb", n3)
@@ -77,8 +77,8 @@ def tile_picked_momtop2lse_none_po_kernel(
 
         ident = sb("ident", [P, P], F32)
         make_identity(nc, ident[:])
-        def gather_words(name, lst):
-            words = sb(name, [P, S], U32)
+        def gather_words(name, lst, tag=None):
+            words = sb(name, [P, S], U32, tag=tag)
             nc.vector.tensor_copy(
                 words[:].rearrange("p (t b e) -> p b t e", t=PACK, e=8), xw[:].bitcast(U32).indirect(lst[:])
             )
@@ -105,11 +105,11 @@ def tile_picked_momtop2lse_none_po_kernel(
         def negate(dst, src):
             nc.scalar.activation(dst, src, ACT.Copy, scale=-1.0)
 
-        def quantize(codes, scales, grouped, c0, c1):
+        def quantize(codes, scales, c0, c1, grouped):
             nc.vector.quantize_mx(
                 out=codes[:, c0:c1].bitcast(FP8X4),
                 scales=scales[:, c0:c1],
-                in_=grouped[:, c0:c1, :].rearrange("p c t -> p (c t)"),
+                in_=grouped.rearrange("p c t -> p (c t)"),
             )
 
         def product(acc, l_codes, l_scales, t, r_codes, r_scales):
@@ -124,13 +124,15 @@ def tile_picked_momtop2lse_none_po_kernel(
             )
 
         xa_listed = gather_scales("xa_scales", offs_sb)
+        xb_listed = gather_scales("xb_scales", two_sb)
         xa_scales = deal_scales("xa_scales", xa_listed)
-        wa_bf = sb("wa_bf", [P, H, PACK], BF16)
+        xb_scales = deal_scales("xb_scales", xb_listed)
         wa_codes = sb("wa_codes", [P, H], U32)
         wa_scales = sb("wa_scales", [P, H], U8)
         for h in range(2):
-            interleave(negate, wa_bf[:, h * HALF : (h + 1) * HALF, :], wa_raw[h][:])
-            quantize(wa_codes, wa_scales, wa_bf, h * HALF, (h + 1) * HALF)
+            wa_bf = sb("wa_bf%d" % h, [P, HALF, PACK], BF16)
+            interleave(negate, wa_bf[:], wa_raw[h][:])
+            quantize(wa_codes, wa_scales, h * HALF, (h + 1) * HALF, wa_bf[:])
         g_ps = bank(0, "g_ps")
         nc.tensor.transpose(g_ps[:, 0:P], g_rows[:], ident[:])
         g_cols = sb("g_cols", [P, 2 * PACK], F32, tag="wa_raw1")
@@ -139,10 +141,8 @@ def tile_picked_momtop2lse_none_po_kernel(
         nc.scalar.activation(gt_abs[:], g_cols[:, 0:PACK], ACT.Abs)
 
         xa_words = gather_words("xa_words", offs_sb)
-        xb_words = gather_words("xb_words", two_sb)
-        xb_listed = gather_scales("xb_scales", two_sb)
-        xb_scales = deal_scales("xb_scales", xb_listed)
-        gt_step = sb("gt_step", [P, PACK], F32, tag="xb_scales_listed")
+        xb_words = gather_words("xb_words", two_sb, tag="wa_bf1")
+        gt_step = sb("gt_step", [P, PACK], F32, tag="xw")
         nc.vector.tensor_scalar(gt_step[:], g_cols[:, 0:PACK], 0.0, 2.0, ALU.is_ge, ALU.mult)
         gi_signed = sb("gi_signed", [P, PACK], F32)
         nc.vector.scalar_tensor_tensor(gi_signed[:], gt_step[:], -1.0, g_cols[:, PACK:], ALU.add, ALU.mult)
@@ -159,52 +159,47 @@ def tile_picked_momtop2lse_none_po_kernel(
 
         c1 = sb("c1", [P, PACK, H], F32)
         z_bf = sb("z_bf", [P, H, PACK], BF16)
-        z_dealt = z_bf[:].rearrange("p (u m) t -> p m t u", u=PACK)
 
-        def look(t, lst, c0, c1):
-            return a_win[t][:].indirect(cols_of(lst, c0, c1))
+        def look(t, lst):
+            return a_win[t][:].indirect(lst[:])
 
-        def turn(acc, terms, col0):
-            slots = acc[:].rearrange("p (t c) -> p t c", t=PACK)
-            for i, term in enumerate(terms):
-                for t in range(PACK):
-                    nc.tensor.matmul(
-                        slots[:, t, :],
-                        term[:, t, col0 : col0 + P],
-                        ident[:],
-                        start=(i == 0 and t == 0),
-                        stop=(i == len(terms) - 1 and t == PACK - 1),
-                        is_transpose=True,
-                    )
+        def turn(acc, t, term, first, last):
+            nc.tensor.matmul(
+                acc[:, t * P : (t + 1) * P],
+                term,
+                ident[:],
+                start=first and t == 0,
+                stop=last and t == PACK - 1,
+                is_transpose=True,
+            )
 
-        def block(name, tag=None):
-            return sb(name, [P, PACK, P], F32, tag=tag)
+        def turn_block(acc, rows, j, first, last):
+            for t in range(PACK):
+                turn(acc, t, rows[:, t, j * P : (j + 1) * P], first, last)
 
-        def by_tile(row):
-            return row.rearrange("p (t c) -> p t c", t=PACK)
-
-        def flat(tile):
-            return tile[:].rearrange("p t c -> p (t c)")
+        def turn_back(acc, turned, first, last):
+            for t in range(PACK):
+                turn(acc, t, turned[:, t * P : (t + 1) * P], first, last)
 
         for t in range(PACK):
-            nc.vector.tensor_copy(c1[:, t, :], look(t, n1_sb, 0, H))
+            nc.vector.tensor_copy(c1[:, t, :], look(t, n1_sb))
 
         wb_codes = sb("wb_codes", [P, N], U32)
         wb_scales = sb("wb_scales", [P, N], U8)
-        quantize(wb_codes, wb_scales, wb_bf, 0, N)
-        diffs = sb("diffs", [P, PACK, H + HALF], F32, tag="turns")
-        dc, ec = diffs[:, :, 0:H], diffs[:, :, H:]
+        quantize(wb_codes, wb_scales, 0, N, wb_bf[:])
+        diffs = sb("diffs", [P, PACK, 2 * H], F32, tag="turns")
+        dc, third = diffs[:, :, 0:H], diffs[:, :, H:]
         for t in range(PACK):
-            nc.vector.tensor_tensor(dc[:, t, :], look(t, n2_sb, 0, H), c1[:, t, :], ALU.subtract)
+            nc.vector.tensor_tensor(dc[:, t, :], look(t, n2_sb), c1[:, t, :], ALU.subtract)
 
-        half_b1 = sb("half_b1", [P, 2, N], F32, tag="wb_raw")
-        for j in range(2):
+        half_b1 = sb("half_b1", [P, TURNED, N], F32, tag="wb_raw")
+        for j in range(TURNED):
             acc = bank(j, "c1_ps%d" % j)
-            turn(acc, [c1], j * P)
+            turn_block(acc, c1, j, True, True)
             nc.scalar.activation(half_b1[:, j, :], acc[:], ACT.Copy, scale=-0.5)
 
-        shared = sb("shared", [P, PACK, 2 * N], F32)
-        z2_rows = shared[:, :, HALF : HALF + N]
+        shared = sb("shared", [P, PACK, 4 * N], F32)
+        z2_rows = shared[:, :, 3 * N - HALF : 3 * N + HALF]
         for t in range(PACK):
             acc = bank(PACK + t, "b_ps%d" % t)
             product(acc, xb_words, xb_scales, t, wb_codes, wb_scales)
@@ -212,71 +207,74 @@ def tile_picked_momtop2lse_none_po_kernel(
         z2_bf = sb("z2_bf", [P, N, PACK], BF16)
         interleave(nc.scalar.copy, z2_bf[:], z2_rows)
 
-        rise = shared[:, 0, :].rearrange("p (t c) -> p t c", t=PACK)
-        gap = shared[:, 1, :].rearrange("p (t c) -> p t c", t=PACK)
-        gap_t = [shared[:, 2 + j, 0:N] for j in range(2)]
-        half_rise = [shared[:, 2 + j, N:] for j in range(2)]
-        nc.scalar.activation(rise, dc[:, :, 0:HALF], ACT.Relu, scale=-1.0)
-        for j in range(2):
-            acc = bank(2 + j, "dc_ps%d" % j)
-            turn(acc, [dc], j * P)
+        z_ps = [bank(j, "z_ps%d" % j) for j in range(TURNED)]
+        for j in range(TURNED):
+            turn_back(z_ps[j], half_b1[:, j, :], True, False)
+
+        wide = TURNED * P
+        rise = shared[:, 0, 0 : 3 * N].rearrange("p (t c) -> p t c", t=PACK)
+        gap = shared[:, 0, 3 * N :].rearrange("p (t c) -> p t c", t=PACK)
+        gap_t = [shared[:, 1 + j, 2 * N : 3 * N] for j in range(TURNED)]
+        half_rise = [shared[:, 1 + j, 3 * N :] for j in range(TURNED)]
+        nc.scalar.activation(rise, dc[:, :, 0:wide], ACT.Relu, scale=-1.0)
+        for j in range(TURNED):
+            acc = bank(3 + j, "dc_ps%d" % j)
+            turn_block(acc, dc, j, True, True)
             nc.scalar.activation(gap_t[j], acc[:], ACT.Abs, scale=0.5)
             nc.scalar.activation(half_rise[j], acc[:], ACT.Relu, scale=-0.5)
-        nc.scalar.activation(gap, dc[:, :, HALF:H], ACT.Abs, scale=0.5)
+        nc.scalar.activation(gap, dc[:, :, wide:H], ACT.Abs, scale=0.5)
 
+        lo = c1[:, :, wide:H]
+        nc.vector.scalar_tensor_tensor(lo, dc[:, :, wide:H], 0.0, lo, ALU.min, ALU.add)
+        over_ps = [bank(b, "over_ps%d" % b) for b in (6, 7, 3)]
+        for j in range(TURNED):
+            turn_block(over_ps[j], rise, j, True, False)
         for t in range(PACK):
-            nc.vector.tensor_tensor(ec[:, t, :], look(t, n3_sb, 0, HALF), c1[:, t, 0:HALF], ALU.subtract)
-        lo = sb("lo", [P, PACK, HALF], F32)
-        nc.vector.scalar_tensor_tensor(lo[:], dc[:, :, HALF:H], 0.0, c1[:, :, HALF:H], ALU.min, ALU.add)
-        over = sb("over", [P, PACK, HALF], F32)
-        for t in range(PACK):
-            nc.vector.tensor_tensor(over[:, t, :], look(t, n3_sb, HALF, H), lo[:, t, :], ALU.subtract)
+            nc.vector.tensor_tensor(third[:, t, :], look(t, n3_sb), c1[:, t, :], ALU.subtract)
+            for j in range(TURNED):
+                turn(over_ps[j], t, third[:, t, j * P : (j + 1) * P], False, True)
+        for j in range(TURNED):
+            turn_back(z_ps[j], half_rise[j], False, False)
 
-        over_ps, low_t, top_t = [], [], []
-        for j in range(2):
-            over_ps.append(bank(PACK + j, "over_ps%d" % j))
-            turn(over_ps[j], [ec, rise], j * P)
-        for j in range(2):
-            low_t.append(block("low_t%d" % j))
-            nc.vector.scalar_tensor_tensor(flat(low_t[j]), over_ps[j][:], 0.5, gap_t[j], ALU.mult, ALU.min)
-        for j in range(2):
-            top_t.append(block("top_t%d" % j))
-            nc.vector.scalar_tensor_tensor(flat(top_t[j]), over_ps[j][:], -1.0, flat(low_t[j]), ALU.mult, ALU.max)
-        for j in range(2):
-            acc = bank(6 + j, "z_ps%d" % j)
-            turn(acc, [by_tile(half_b1[:, j, :]), by_tile(half_rise[j]), top_t[j]], 0)
-            nc.scalar.copy(
-                z_dealt[:, 32 * j : 32 * j + 32, :, :], acc[:].rearrange("p (t m u) -> p m t u", t=PACK, u=PACK)
-            )
-
-        low, top, z = [], [], []
-        for j in range(2):
-            low.append(block("low%d" % j, tag="low_t%d" % j))
-            cs = slice(j * P, (j + 1) * P)
-            nc.vector.scalar_tensor_tensor(low[j][:], over[:, :, cs], 0.5, gap[:, :, cs], ALU.mult, ALU.min)
-        for j in range(2):
-            top.append(block("top%d" % j))
-            cs = slice(j * P, (j + 1) * P)
-            nc.vector.scalar_tensor_tensor(top[j][:], over[:, :, cs], -1.0, low[j][:], ALU.mult, ALU.max)
         z2_codes = sb("z2_codes", [P, N], U32)
         z2_scales = sb("z2_scales", [P, N], U8)
-        quantize(z2_codes, z2_scales, z2_bf, 0, N)
-        for j, engine_copy in enumerate((nc.scalar.copy, nc.vector.tensor_copy)):
-            z.append(block("z%d" % j))
-            cs = slice(j * P, (j + 1) * P)
-            nc.vector.scalar_tensor_tensor(z[j][:], lo[:, :, cs], -0.5, top[j][:], ALU.mult, ALU.add)
-        for j, engine_copy in enumerate((nc.scalar.copy, nc.vector.tensor_copy)):
-            engine_copy(
-                z_dealt[:, 64 + 32 * j : 96 + 32 * j, :, :], z[j][:].rearrange("p t (m u) -> p m t u", u=PACK)
+        quantize(z2_codes, z2_scales, 0, N, z2_bf[:])
+
+        low_t = [sb("low_t%d" % j, [P, N], F32) for j in range(TURNED)]
+        top_t = [sb("top_t%d" % j, [P, N], F32) for j in range(TURNED)]
+        for j in range(TURNED):
+            nc.vector.scalar_tensor_tensor(low_t[j][:], over_ps[j][:], 0.5, gap_t[j], ALU.mult, ALU.min)
+        for j in range(TURNED):
+            nc.vector.scalar_tensor_tensor(top_t[j][:], over_ps[j][:], -1.0, low_t[j][:], ALU.mult, ALU.max)
+            turn_back(z_ps[j], top_t[j], False, True)
+            nc.scalar.copy(
+                z_bf[:].rearrange("p (u m) t -> p u m t", u=PACK)[:, :, 32 * j : 32 * j + 32, :],
+                z_ps[j][:].rearrange("p (t m u) -> p u m t", t=PACK, u=PACK),
             )
+
+        over = third[:, :, wide:H]
+        low = sb("low", [P, PACK, P], F32, tag="low_t0")
+        top = sb("top", [P, PACK, P], F32)
+        z = sb("z", [P, PACK, P], F32)
+        pairs = (slice(0, 2), slice(2, 4))
+        for ts in pairs:
+            nc.vector.scalar_tensor_tensor(low[:, ts, :], over[:, ts, :], 0.5, gap[:, ts, :], ALU.mult, ALU.min)
+        for ts in pairs:
+            nc.vector.scalar_tensor_tensor(top[:, ts, :], over[:, ts, :], -1.0, low[:, ts, :], ALU.mult, ALU.max)
+        for ts in pairs:
+            nc.vector.scalar_tensor_tensor(z[:, ts, :], lo[:, ts, :], -0.5, top[:, ts, :], ALU.mult, ALU.add)
+        nc.vector.tensor_copy(
+            z_bf[:].rearrange("p (u m) t -> p m t u", u=PACK)[:, 32 * TURNED :, :, :],
+            z[:].rearrange("p t (m u) -> p m t u", u=PACK),
+        )
 
         z_codes = sb("z_codes", [P, H], U32)
         z_scales = sb("z_scales", [P, H], U8)
         cv_ps = []
         for u in range(PACK):
-            quantize(z_codes, z_scales, z_bf, u * P, (u + 1) * P)
+            quantize(z_codes, z_scales, u * P, (u + 1) * P, z_bf[:, u * P : (u + 1) * P, :])
         for u in range(PACK):
-            acc = bank(u, "cv_ps%d" % u)
+            acc = bank(PACK + u, "cv_ps%d" % u)
             product(acc, z_codes, z_scales, u, z2_codes, z2_scales)
             cv_ps.append(acc)
 
@@ -314,7 +312,7 @@ def tile_picked_momtop2lse_none_po_kernel(
             nc.sync.dma_start(out_rows[:, u, c0:c1], res[:, u, c0:c1])
 
         def planes(c0, c1):
-            quantize(o_codes, o_scales, res_bf, c0, c1)
+            quantize(o_codes, o_scales, c0, c1, res_bf[:, c0:c1, :])
             nc.sync.dma_start(words_out[:, c0:c1], o_codes[:, c0:c1].bitcast(I32))
 
         finish(1, 0, N)

from contextlib import ExitStack

import concourse.mybir as mybir
from concourse.masks import make_identity

K, T, S, H, N = 512, 2048, 512, 512, 512
FLOPS = 2 * S * K * H + 2 * S * K * N + 2 * H * S * N

F32 = mybir.dt.float32
BF16 = mybir.dt.bfloat16
I32 = mybir.dt.int32
U32 = mybir.dt.uint32
U16 = mybir.dt.uint16
U8 = mybir.dt.uint8
FP8X4 = mybir.dt.float8_e4m3fn_x4
ALU = mybir.AluOpType
ACT = mybir.ActivationFunctionType

P = 128
PACK = 4
HALF = 256
PER_COL = 16
TURNED = 3


def tile_picked_momtop2lse_none_po_kernel(
    tc, x_words, x_scales, wa, wb, gt, gi, offs, two, n1, n2, n3, n4, n5, out_0, out_1, out_2
):
    nc = tc.nc
    with ExitStack() as ctx:
        lists = ctx.enter_context(tc.tile_pool(name="lists", bufs=1))
        keep = ctx.enter_context(tc.tile_pool(name="keep", bufs=1))
        psum = ctx.enter_context(tc.psum_pool(name="psum", bufs=1))

        def sb(name, shape, dtype, tag=None):
            return keep.tile(shape, dtype, name=name, tag=tag or name, align_bytes=64)

        def bank(b, name):
            return psum.tile([P, 512], F32, name=name, tag="bank%d" % b)

        def load_list(name, src):
            tile = lists.tile([P, S // PER_COL], U16, name=name)
            nc.sync.dma_start(tile[:], src)
            return tile

        def cols_of(tile, c0, c1):
            return tile[:, c0 // PER_COL : c1 // PER_COL]

        xs = sb("xs", [P, T], U8)
        nc.gpsimd.memset(xs[:].bitcast(I32), 0)
        offs_sb = load_list("offs_sb", offs)
        two_sb = load_list("two_sb", two)
        for q in range(4):
            nc.sync.dma_start(
                xs[32 * q : 32 * q + 4, :].bitcast(I32), x_scales[0, 4 * q : 4 * q + 4, :].bitcast(I32)
            )
        wa_rows = wa.rearrange("(p j) c -> p j c", j=PACK)
        wa_raw = [sb("wa_raw%d" % h, [P, PACK, HALF], F32) for h in range(2)]
        nc.sync.dma_start(wa_raw[0][:], wa_rows[:, :, 0:HALF])
        xw = sb("xw", [P, T], I32)
        nc.sync.dma_start(xw[:], x_words[0].rearrange("p c r -> p (c r)").bitcast(I32))
        nc.sync.dma_start(wa_raw[1][:], wa_rows[:, :, HALF:H])
        g_rows = sb("g_rows", [P, P], F32)
        nc.vector.memset(g_rows[:], 0.0)
        for r, src in ((0, gt), (PACK, gi)):
            nc.sync.dma_start(
                g_rows[r : r + PACK, :].rearrange("t (b e) -> t b e", e=8),
                src.rearrange("(b t e) o -> t b (e o)", t=PACK, e=8),
            )
        n1_sb = load_list("n1_sb", n1)
        n2_sb = load_list("n2_sb", n2)
        n3_sb = load_list("n3_sb", n3)
        wb_raw = sb("wb_raw", [P, PACK, N], F32)
        nc.sync.dma_start(wb_raw[:], wb.rearrange("(p j) c -> p j c", j=PACK))
        n4_sb = load_list("n4_sb", n4)
        n5_sb = load_list("n5_sb", n5)

        ident = sb("ident", [P, P], F32)
        make_identity(nc, ident[:])
        def gather_words(name, lst, tag=None):
            words = sb(name, [P, S], U32, tag=tag)
            nc.vector.tensor_copy(
                words[:].rearrange("p (t b e) -> p b t e", t=PACK, e=8), xw[:].bitcast(U32).indirect(lst[:])
            )
            return words

        def gather_scales(name, lst):
            listed = sb(name + "_listed", [P, S], U8)
            nc.vector.tensor_copy(listed[:], xs[:].indirect(lst[:]))
            return listed

        def deal_scales(name, listed):
            dealt = sb(name, [P, S], U8)
            nc.vector.tensor_copy(
                dealt[:].bitcast(I32).rearrange("p (t b e) -> p t b e", t=PACK, e=2),
                listed[:].bitcast(I32).rearrange("p (b t e) -> p t b e", t=PACK, e=2),
            )
            return dealt

        def interleave(engine_copy, dst, src):
            engine_copy(
                dst.rearrange("p (c i) t -> p c t i", i=4), src.rearrange("p t (c i) -> p c t i", i=4)
            )

        def negate(dst, src):
            nc.scalar.activation(dst, src, ACT.Copy, scale=-1.0)

        def quantize(codes, scales, c0, c1, grouped):
            nc.vector.quantize_mx(
                out=codes[:, c0:c1].bitcast(FP8X4),
                scales=scales[:, c0:c1],
                in_=grouped.rearrange("p c t -> p (c t)"),
            )

        def product(acc, l_codes, l_scales, t, r_codes, r_scales):
            nc.tensor.matmul_mx(
                out=acc[:],
                lhsT=l_codes[:, t * P : (t + 1) * P].bitcast(FP8X4),
                lhsT_scale=l_scales[:, t * P : (t + 1) * P],
                rhs=r_codes[:].bitcast(FP8X4),
                rhs_scale=r_scales[:],
                start=True,
                stop=True,
            )

        xa_listed = gather_scales("xa_scales", offs_sb)
        xb_listed = gather_scales("xb_scales", two_sb)
        xa_scales = deal_scales("xa_scales", xa_listed)
        xb_scales = deal_scales("xb_scales", xb_listed)
        wa_codes = sb("wa_codes", [P, H], U32)
        wa_scales = sb("wa_scales", [P, H], U8)
        for h in range(2):
            wa_bf = sb("wa_bf%d" % h, [P, HALF, PACK], BF16)
            interleave(negate, wa_bf[:], wa_raw[h][:])
            quantize(wa_codes, wa_scales, h * HALF, (h + 1) * HALF, wa_bf[:])
        g_ps = bank(0, "g_ps")
        nc.tensor.transpose(g_ps[:, 0:P], g_rows[:], ident[:])
        g_cols = sb("g_cols", [P, 2 * PACK], F32, tag="wa_raw1")
        nc.scalar.copy(g_cols[:], g_ps[:, 0 : 2 * PACK])
        gt_abs = sb("gt_abs", [P, PACK], F32, tag="turns")
        nc.scalar.activation(gt_abs[:], g_cols[:, 0:PACK], ACT.Abs)

        xa_words = gather_words("xa_words", offs_sb)
        xb_words = gather_words("xb_words", two_sb, tag="wa_bf1")
        gt_step = sb("gt_step", [P, PACK], F32, tag="xw")
        nc.vector.tensor_scalar(gt_step[:], g_cols[:, 0:PACK], 0.0, 2.0, ALU.is_ge, ALU.mult)
        gi_signed = sb("gi_signed", [P, PACK], F32)
        nc.vector.scalar_tensor_tensor(gi_signed[:], gt_step[:], -1.0, g_cols[:, PACK:], ALU.add, ALU.mult)
        a_win = []
        for t in range(PACK):
            acc = bank(t, "a_ps%d" % t)
            product(acc, xa_words, xa_scales, t, wa_codes, wa_scales)
            win = sb("a_win%d" % t, [P, 2 * H], F32)
            nc.scalar.activation(win[:, 0:H], acc[:], ACT.Copy, scale=gt_abs[:, t : t + 1])
            a_win.append(win)

        wb_bf = sb("wb_bf", [P, N, PACK], BF16, tag="turns")
        interleave(nc.scalar.copy, wb_bf[:], wb_raw[:])

        c1 = sb("c1", [P, PACK, H], F32)
        z_bf = sb("z_bf", [P, H, PACK], BF16)

        def look(t, lst):
            return a_win[t][:].indirect(lst[:])

        def turn(acc, t, term, first, last):
            nc.tensor.matmul(
                acc[:, t * P : (t + 1) * P],
                term,
                ident[:],
                start=first and t == 0,
                stop=last and t == PACK - 1,
                is_transpose=True,
            )

        def turn_block(acc, rows, j, first, last):
            for t in range(PACK):
                turn(acc, t, rows[:, t, j * P : (j + 1) * P], first, last)

        def turn_back(acc, turned, first, last):
            for t in range(PACK):
                turn(acc, t, turned[:, t * P : (t + 1) * P], first, last)

        for t in range(PACK):
            nc.vector.tensor_copy(c1[:, t, :], look(t, n1_sb))

        wb_codes = sb("wb_codes", [P, N], U32)
        wb_scales = sb("wb_scales", [P, N], U8)
        quantize(wb_codes, wb_scales, 0, N, wb_bf[:])
        diffs = sb("diffs", [P, PACK, 2 * H], F32, tag="turns")
        dc, third = diffs[:, :, 0:H], diffs[:, :, H:]
        for t in range(PACK):
            nc.vector.tensor_tensor(dc[:, t, :], look(t, n2_sb), c1[:, t, :], ALU.subtract)

        half_b1 = sb("half_b1", [P, TURNED, N], F32, tag="wb_raw")
        for j in range(TURNED):
            acc = bank(j, "c1_ps%d" % j)
            turn_block(acc, c1, j, True, True)
            nc.scalar.activation(half_b1[:, j, :], acc[:], ACT.Copy, scale=-0.5)

        shared = sb("shared", [P, PACK, 4 * N], F32)
        z2_rows = shared[:, :, 3 * N - HALF : 3 * N + HALF]
        for t in range(PACK):
            acc = bank(PACK + t, "b_ps%d" % t)
            product(acc, xb_words, xb_scales, t, wb_codes, wb_scales)
            nc.scalar.activation(z2_rows[:, t, :], acc[:], ACT.Copy, scale=gi_signed[:, t : t + 1])
        z2_bf = sb("z2_bf", [P, N, PACK], BF16)
        interleave(nc.scalar.copy, z2_bf[:], z2_rows)

        z_ps = [bank(j, "z_ps%d" % j) for j in range(TURNED)]
        for j in range(TURNED):
            turn_back(z_ps[j], half_b1[:, j, :], True, False)

        wide = TURNED * P
        rise = shared[:, 0, 0 : 3 * N].rearrange("p (t c) -> p t c", t=PACK)
        gap = shared[:, 0, 3 * N :].rearrange("p (t c) -> p t c", t=PACK)
        gap_t = [shared[:, 1 + j, 2 * N : 3 * N] for j in range(TURNED)]
        half_rise = [shared[:, 1 + j, 3 * N :] for j in range(TURNED)]
        nc.scalar.activation(rise, dc[:, :, 0:wide], ACT.Relu, scale=-1.0)
        for j in range(TURNED):
            acc = bank(3 + j, "dc_ps%d" % j)
            turn_block(acc, dc, j, True, True)
            nc.scalar.activation(gap_t[j], acc[:], ACT.Abs, scale=0.5)
            nc.scalar.activation(half_rise[j], acc[:], ACT.Relu, scale=-0.5)
        nc.scalar.activation(gap, dc[:, :, wide:H], ACT.Abs, scale=0.5)

        lo = c1[:, :, wide:H]
        nc.vector.scalar_tensor_tensor(lo, dc[:, :, wide:H], 0.0, lo, ALU.min, ALU.add)
        over_ps = [bank(b, "over_ps%d" % b) for b in (6, 7, 3)]
        for j in range(TURNED):
            turn_block(over_ps[j], rise, j, True, False)
        for t in range(PACK):
            nc.vector.tensor_tensor(third[:, t, :], look(t, n3_sb), c1[:, t, :], ALU.subtract)
            for j in range(TURNED):
                turn(over_ps[j], t, third[:, t, j * P : (j + 1) * P], False, True)
        for j in range(TURNED):
            turn_back(z_ps[j], half_rise[j], False, False)

        z2_codes = sb("z2_codes", [P, N], U32)
        z2_scales = sb("z2_scales", [P, N], U8)
        quantize(z2_codes, z2_scales, 0, N, z2_bf[:])

        low_t = [sb("low_t%d" % j, [P, N], F32) for j in range(TURNED)]
        top_t = [sb("top_t%d" % j, [P, N], F32) for j in range(TURNED)]
        for j in range(TURNED):
            nc.vector.scalar_tensor_tensor(low_t[j][:], over_ps[j][:], 0.5, gap_t[j], ALU.mult, ALU.min)
        for j in range(TURNED):
            nc.vector.scalar_tensor_tensor(top_t[j][:], over_ps[j][:], -1.0, low_t[j][:], ALU.mult, ALU.max)
            turn_back(z_ps[j], top_t[j], False, True)
            nc.scalar.copy(
                z_bf[:].rearrange("p (u m) t -> p u m t", u=PACK)[:, :, 32 * j : 32 * j + 32, :],
                z_ps[j][:].rearrange("p (t m u) -> p u m t", t=PACK, u=PACK),
            )

        over = third[:, :, wide:H]
        low = sb("low", [P, PACK, P], F32, tag="low_t0")
        top = sb("top", [P, PACK, P], F32)
        z = sb("z", [P, PACK, P], F32)
        pairs = (slice(0, 2), slice(2, 4))
        for ts in pairs:
            nc.vector.scalar_tensor_tensor(low[:, ts, :], over[:, ts, :], 0.5, gap[:, ts, :], ALU.mult, ALU.min)
        for ts in pairs:
            nc.vector.scalar_tensor_tensor(top[:, ts, :], over[:, ts, :], -1.0, low[:, ts, :], ALU.mult, ALU.max)
        for ts in pairs:
            nc.vector.scalar_tensor_tensor(z[:, ts, :], lo[:, ts, :], -0.5, top[:, ts, :], ALU.mult, ALU.add)
        nc.vector.tensor_copy(
            z_bf[:].rearrange("p (u m) t -> p m t u", u=PACK)[:, 32 * TURNED :, :, :],
            z[:].rearrange("p t (m u) -> p m t u", u=PACK),
        )

        z_codes = sb("z_codes", [P, H], U32)
        z_scales = sb("z_scales", [P, H], U8)
        cv_ps = []
        for u in range(PACK):
            quantize(z_codes, z_scales, u * P, (u + 1) * P, z_bf[:, u * P : (u + 1) * P, :])
        for u in range(PACK):
            acc = bank(PACK + u, "cv_ps%d" % u)
            product(acc, z_codes, z_scales, u, z2_codes, z2_scales)
            cv_ps.append(acc)

        ex = sb("ex", [P, PACK, N], F32)
        both = sb("both", [P, PACK, N], F32)
        logs = sb("logs", [P, PACK, N], F32)
        res = sb("res", [P, PACK, N], F32)
        ex_win = [sb("ex_win%d" % u, [P, 2 * N], F32) for u in range(PACK)]
        neg_win = [sb("neg_win%d" % u, [P, 2 * N], F32) for u in range(PACK)]

        def neg_copy(u):
            nc.vector.tensor_scalar(neg_win[u][:, 0:N], cv_ps[u][:], -0.0625, None, ALU.mult)

        neg_copy(1)
        neg_copy(2)
        for u in range(PACK):
            nc.scalar.activation(ex_win[u][:, 0:N], cv_ps[u][:], ACT.Exp, scale=0.0625)
            nc.scalar.activation(ex[:, u, :], cv_ps[u][:], ACT.Exp, scale=0.0625)
            nc.vector.tensor_tensor(both[:, u, :], ex_win[u][:].indirect(n4_sb[:]), ex[:, u, :], ALU.add)
        for u in (1, 2, 0, 3):
            if u in (0, 3):
                nc.scalar.activation(neg_win[u][:, 0:N], cv_ps[u][:], ACT.Copy, scale=-0.0625)
            nc.scalar.activation(logs[:, u, :], both[:, u, :], ACT.Ln)

        out_rows = out_0.rearrange("(p u) c -> p u c", u=PACK)
        res_bf = sb("res_bf", [P, N, PACK], BF16)
        o_codes = sb("o_codes", [P, N], U32)
        o_scales = sb("o_scales", [P, N], U8)
        words_out = out_1[0].rearrange("p c r -> p (c r)").bitcast(I32)

        def finish(u, c0, c1):
            nc.vector.tensor_tensor(
                res[:, u, c0:c1], neg_win[u][:].indirect(cols_of(n5_sb, c0, c1)), logs[:, u, c0:c1], ALU.add
            )
            nc.sync.dma_start(out_rows[:, u, c0:c1], res[:, u, c0:c1])

        def planes(c0, c1):
            quantize(o_codes, o_scales, c0, c1, res_bf[:, c0:c1, :])
            nc.sync.dma_start(words_out[:, c0:c1], o_codes[:, c0:c1].bitcast(I32))

        finish(1, 0, N)
        finish(2, 0, N)
        finish(0, 0, HALF)
        finish(3, 0, HALF)
        interleave(nc.scalar.copy, res_bf[:, 0:HALF, :], res[:, :, 0:HALF])
        finish(0, HALF, N)
        finish(3, HALF, N)
        split = HALF + 80
        interleave(nc.scalar.copy, res_bf[:, HALF:split, :], res[:, :, HALF:split])
        interleave(nc.vector.tensor_copy, res_bf[:, split:N, :], res[:, :, split:N])
        planes(0, HALF)
        planes(HALF, N)
        for q in range(4):
            queue = nc.scalar if q % 2 else nc.sync
            queue.dma_start(
                out_2[0, 4 * q : 4 * q + 4, :].bitcast(I32), o_scales[32 * q : 32 * q + 4, :].bitcast(I32)
            )
